import numpy as np
import ml_dtypes


def mxq(x, axis, fmt="e4m3"):
    dtype, down = {"e4m3": (ml_dtypes.float8_e4m3fn, 7), "e5m2": (ml_dtypes.float8_e5m2, 14)}[fmt]
    v = np.moveaxis(np.asarray(x, np.float32).astype(ml_dtypes.bfloat16).astype(np.float64), axis, -1)
    blocks = v.reshape(v.shape[:-1] + (-1, 32))
    amax = np.abs(blocks).max(-1, keepdims=True)
    byte = np.maximum(np.where(amax > 0, np.frexp(amax)[1] - 1 + 127, 0) - down, 1)
    scale = np.exp2(byte - 127.0)
    codes = (blocks / scale).astype(np.float32).astype(dtype).astype(np.float64)
    return np.moveaxis((codes * scale).reshape(v.shape), -1, axis)


WIDE = False


def mx_kscale(k):
    if not WIDE:
        return np.ones(k)
    levels = np.array([10, -10, 5, -5, 0])
    if k % 512:
        return np.exp2(np.random.permutation(np.resize(levels, k // 32))).repeat(32)
    a = np.empty((k // 512, 16))
    for p in range(k // 512):
        a[p, :8] = np.random.permutation(np.resize(levels, 8))
        for g in range(8):
            far = levels[np.abs(levels - a[p, g]) >= 10]
            a[p, g + 8] = far[np.random.randint(len(far))]
    return np.exp2(a.ravel()).repeat(32)


def f64(x):
    return np.asarray(x).astype(np.float64)


def striped(idx):
    return np.tile(idx.reshape(-1, 16).T, (8, 1)).astype(np.uint16)


def unstriped(offs):
    return offs[:16].T.reshape(-1).astype(np.int64)


E2M1 = np.array([0.0, 0.5, 1.0, 1.5, 2.0, 3.0, 4.0, 6.0, -0.0, -0.5, -1.0, -1.5, -2.0, -3.0, -4.0, -6.0])


def pack_weight(w, fmt):
    k, n = w.shape
    w = f64(np.asarray(w, np.float32).astype(ml_dtypes.bfloat16)).reshape(k // 32, 32, n)
    amax = np.abs(w).max(1)
    if fmt == "e4m3":
        byte = np.frexp(amax)[1] - 1 + 127 - 7
    else:
        mant, ex = np.frexp(amax / 6.0)
        byte = np.where(mant > 0.5, ex, ex - 1) + 127
    byte = np.clip(np.where(amax > 0, byte, 1), 1, 254)
    scaled = (w * np.exp2(127.0 - byte)[:, None, :]).reshape(k, n).astype(np.float32)
    by_word = np.ascontiguousarray(scaled.reshape(k // 512, 128, 4, n).transpose(0, 1, 3, 2))
    if fmt == "e4m3":
        words = by_word.astype(ml_dtypes.float8_e4m3fn).view(np.uint8)
    else:
        c = by_word.astype(ml_dtypes.float4_e2m1fn).view(np.uint8) & 0xF
        words = (c[..., 0::2] | (c[..., 1::2] << 4)).reshape(k // 512, 128, 2 * n)
    return np.ascontiguousarray(words), np.ascontiguousarray(byte.astype(np.uint8).reshape(k // 512, 16, n))


def unpack_weight(words, scales, fmt):
    g, _, n = scales.shape
    words = np.ascontiguousarray(words).reshape(g, 128, n, -1)
    if fmt == "e4m3":
        vals = words.view(ml_dtypes.float8_e4m3fn).astype(np.float64)
    else:
        nib = np.empty((g, 128, n, 4), np.uint8)
        nib[..., 0::2] = words & 0xF
        nib[..., 1::2] = words >> 4
        vals = E2M1[nib]
    vals = vals * np.repeat(np.exp2(scales.astype(np.float64) - 127.0), 8, axis=1)[..., None]
    return vals.transpose(0, 1, 3, 2).reshape(g * 512, n)


def gelu(v):
    return 0.5 * v * (1.0 + np.tanh(np.sqrt(2.0 / np.pi) * (v + 0.044715 * v**3)))


def bf(x):
    return np.asarray(x, np.float32).astype(ml_dtypes.bfloat16)


def planes(Y):
    n, m = Y.shape
    b = f64(bf(Y)).reshape(n // 32, 32, m)
    amax = np.abs(b).max(1)
    byte = np.clip(np.where(amax > 0, np.frexp(amax)[1] - 1 + 127 - 7, 1), 1, 254)
    codes = (b * np.exp2(127.0 - byte)[:, None, :]).reshape(n, m).astype(np.float32).astype(ml_dtypes.float8_e4m3fn).view(np.uint8)
    words = codes.reshape(n // 512, 128, 4, m).transpose(0, 1, 3, 2)
    return np.ascontiguousarray(words), np.ascontiguousarray(byte.astype(np.uint8).reshape(n // 512, 16, m))


K, T, H, S, P = 1536, 2048, 512, 1024, 512


def setup_inputs():
    n = np.random.standard_normal
    s = mx_kscale(K)[:, None]
    u = mx_kscale(H)[:, None]
    tab_words, tab_scales = pack_weight(n((K, T)) * s, "e4m3")
    w2_words, w2_scales = pack_weight(1.15 * n((H, H)) / np.sqrt(H) / u, "e2m1")
    return {
        "tab_words": tab_words,
        "tab_scales": tab_scales,
        "offs": striped(np.random.permutation(T)[:S]),
        "pos1": striped(np.random.permutation(S)[:P]),
        "pos2": striped(np.random.permutation(S)[:P]),
        "w1": (1.1 * n((K, H)) / np.sqrt(K) / s).astype(np.float32),
        "lot": (0.8 * n((H, S))).astype(np.float32),
        "tgain": (np.random.uniform(0.5, 1.5, H) * u[:, 0]).astype(np.float32),
        "w2_words": w2_words,
        "w2_scales": w2_scales,
        "sharp": np.random.uniform(0.6, 3.0, H).astype(np.float32),
        "thr": n(H).astype(np.float32),
        "mgain": (np.random.uniform(0.5, 1.5, H) * u[:, 0]).astype(np.float32),
        "w3": (1.8 * n((H, H)) / np.sqrt(H) / u).astype(np.float32),
        "ygain": np.exp(0.8 * n(H)).astype(np.float32),
    }


def reference(tab_words, tab_scales, offs, pos1, pos2, w1, lot, tgain,
              w2_words, w2_scales, sharp, thr, mgain, w3, ygain):
    v = unpack_weight(tab_words, tab_scales, "e4m3")[:, unstriped(offs)]
    g = (mxq(f64(w1), 0, "e4m3").T @ v) + f64(lot)
    f = mxq(f64(tgain)[:, None] * np.tanh(g), 0, "e4m3")
    h = unpack_weight(w2_words, w2_scales, "e2m1").T @ f
    a = 1.0 / (1.0 + np.exp(-(f64(sharp)[:, None] * h[:, unstriped(pos1)] + f64(thr)[:, None])))
    c = g[:, unstriped(pos2)]
    d = mxq(f64(mgain)[:, None] * (a * c), 0, "e4m3")
    y = f64(ygain)[:, None] * np.maximum(mxq(f64(w3), 0, "e4m3").T @ d, c)
    words, scales = planes(y)
    return y, words, scales

@@ -1,0 +1,290 @@
+from contextlib import ExitStack
+
+import concourse.mybir as mybir
+
+K, T, H, S, M = 1536, 2048, 512, 1024, 512
+FLOPS = 2 * (K * H * S + H * H * S + H * H * M)
+
+F32 = mybir.dt.float32
+BF16 = mybir.dt.bfloat16
+I32 = mybir.dt.int32
+U32 = mybir.dt.uint32
+U16 = mybir.dt.uint16
+U8 = mybir.dt.uint8
+FP8X4 = mybir.dt.float8_e4m3fn_x4
+FP4X4 = mybir.dt.float4_e2m1fn_x4
+ALU = mybir.AluOpType
+ACT = mybir.ActivationFunctionType
+
+P = 128
+PACK = 4
+PASSES = K // (P * PACK)
+BANK = 512
+SH = S // 2
+SQ = S // 4
+MH = M // 2
+MQ = M // 4
+LIST_ROWS = 16
+
+
+def tile_list_gelcard_reaction_features_kernel(
+    tc, tab_words, tab_scales, offs, pos1, pos2, w1, lot, tgain, w2_words, w2_scales,
+    sharp, thr, mgain, w3, ygain, out_0, out_1, out_2,
+):
+    nc = tc.nc
+    with ExitStack() as ctx:
+        sb = ctx.enter_context(tc.tile_pool(name="sb", bufs=1))
+        ps = ctx.enter_context(tc.psum_pool(name="ps", bufs=1))
+
+        def tile(shape, dtype, name, tag=""):
+            return sb.tile(shape, dtype, name=name, tag=tag or name, align_bytes=64)
+
+        def bank(shape, name, index):
+            return ps.tile(shape, F32, name=name, tag="bank%d" % index)
+
+        def deal_columns(engine_copy, grouped, raw, m0, m1):
+            out = grouped[:].rearrange("p (t m j) -> p m j t", t=PACK, j=PACK)[:, m0:m1]
+            engine_copy(out=out, in_=raw[:].rearrange("p j (m t) -> p m j t", t=PACK))
+
+        def by_lines(planes):
+            return planes.rearrange("p t (c i) -> p c t i", i=4)
+
+        def woven_by_lines(woven):
+            return woven.rearrange("p (c i t) -> p c t i", i=4, t=PACK)
+
+        offs_sb = tile([P, S // LIST_ROWS], U16, "offs_sb")
+        pos1_sb = tile([P, M // LIST_ROWS], U16, "pos1_sb")
+        pos2_sb = tile([P, M // LIST_ROWS], U16, "pos2_sb")
+        tscale = tile([P, T], U8, "tscale")
+        w2w_raw = tile([P, 2 * H], U8, "w2w_raw")
+        w2s_raw = tile([P, H], U8, "w2s_raw")
+        nc.vector.memset(tscale[:].bitcast(I32), 0)
+        nc.gpsimd.memset(w2s_raw[:].bitcast(I32), 0)
+        twords = [tile([P, T], U32, "twords%d" % a) for a in range(PASSES)]
+        w1_rows = w1.rearrange("(a p j) c -> a p j c", p=P, j=PACK)
+        w1_raw = [tile([P, PACK, H], F32, "w1_raw%d" % a) for a in range(PASSES - 1)]
+        w1_last = [tile([P, PACK, H // 2], F32, "w1_last%d" % u) for u in range(2)]
+        rowvec = {}
+
+        def load_rowvec(name, vec):
+            rowvec[name] = tile([P, PACK], F32, name + "_sb")
+            nc.sync.dma_start(out=rowvec[name][:], in_=vec.rearrange("(p t) -> p t", t=PACK))
+
+        def load_table(a):
+            nc.sync.dma_start(
+                out=twords[a][:].bitcast(I32),
+                in_=tab_words[a].rearrange("p n t -> p (n t)").bitcast(I32),
+            )
+
+        nc.sync.dma_start(offs_sb[:], offs)
+        load_table(0)
+        nc.sync.dma_start(out=w1_raw[0][:], in_=w1_rows[0])
+        for q in range(4):
+            nc.sync.dma_start(
+                out=tscale[32 * q : 32 * q + 4 * PASSES, :].bitcast(I32),
+                in_=tab_scales[:, 4 * q : 4 * q + 4, :].bitcast(I32),
+            )
+        nc.sync.dma_start(pos2_sb[:], pos2)
+        nc.sync.dma_start(pos1_sb[:], pos1)
+        load_table(1)
+        nc.sync.dma_start(out=w2w_raw[:].bitcast(I32), in_=w2_words[0].bitcast(I32))
+        for q in range(4):
+            nc.sync.dma_start(
+                out=w2s_raw[32 * q : 32 * q + 4, :].bitcast(I32),
+                in_=w2_scales[0, 4 * q : 4 * q + 4, :].bitcast(I32),
+            )
+        nc.sync.dma_start(out=w1_raw[1][:], in_=w1_rows[1])
+        load_table(2)
+        for u in range(2):
+            nc.sync.dma_start(out=w1_last[u][:], in_=w1_rows[PASSES - 1][:, :, u * (H // 2) : (u + 1) * (H // 2)])
+        lot_rows = lot.rearrange("(p t) s -> p t s", t=PACK)
+        lot_sb = {}
+        for u in range(2):
+            for t in range(PACK):
+                lot_sb[u, t] = tile([P, SH], F32, "lot%d%d" % (u, t))
+                nc.sync.dma_start(out=lot_sb[u, t][:], in_=lot_rows[:, t, u * SH : (u + 1) * SH])
+            if u == 0:
+                load_rowvec("tgain", tgain)
+        w3_rows = w3.rearrange("(p j) c -> p j c", j=PACK)
+        w3_raw = [tile([P, PACK, H // 2], F32, "w3_raw%d" % u) for u in range(2)]
+        for u in range(2):
+            nc.sync.dma_start(out=w3_raw[u][:], in_=w3_rows[:, :, u * (H // 2) : (u + 1) * (H // 2)])
+        for name, vec in (("mgain", mgain), ("sharp", sharp), ("thr", thr), ("ygain", ygain)):
+            load_rowvec(name, vec)
+
+        vscale = tile([P, S], U8, "vscale")
+        nc.vector.tensor_copy(vscale[:], tscale[:].indirect(offs_sb[:]))
+        vwords = [tile([P, S], U32, "vwords%d" % a) for a in range(PASSES)]
+        w1_codes = [tile([P, H], U32, "w1_codes%d" % a) for a in range(PASSES)]
+        w1_scale = [tile([P, H], U8, "w1_scale%d" % a) for a in range(PASSES)]
+        w2w = tile([P, 2 * H], U8, "w2w")
+        w2s = tile([P, H], U8, "w2s")
+        g_ps = {(u, t): bank([P, BANK], "g_ps%d%d" % (u, t), PACK * u + t) for u in range(2) for t in range(PACK)}
+
+        def first_product(a, u, t):
+            nc.tensor.matmul_mx(
+                out=g_ps[u, t][:],
+                lhsT=w1_codes[a][:, t * P : (t + 1) * P].bitcast(FP8X4),
+                lhsT_scale=w1_scale[a][:, t * P : (t + 1) * P],
+                rhs=vwords[a][:, u * SH : (u + 1) * SH].bitcast(FP8X4),
+                rhs_scale=vscale[4 * a : P, u * SH : (u + 1) * SH],
+                start=(a == 0),
+                stop=(a == PASSES - 1),
+            )
+
+        for a in range(PASSES):
+            nc.vector.tensor_copy(vwords[a][:], twords[a][:].indirect(offs_sb[:]))
+            w1_bf = tile([P, PACK * H], BF16, "w1_bf%d" % a)
+            if a < PASSES - 1:
+                deal_columns(nc.scalar.copy, w1_bf, w1_raw[a], 0, P)
+                nc.vector.quantize_mx(out=w1_codes[a][:].bitcast(FP8X4), scales=w1_scale[a][:], in_=w1_bf[:])
+            else:
+                deal_columns(nc.scalar.copy, w1_bf, w1_last[0], 0, P // 2)
+                deal_columns(nc.vector.tensor_copy, w1_bf, w1_last[1], P // 2, P)
+                for t in range(PACK):
+                    nc.vector.quantize_mx(
+                        out=w1_codes[a][:, t * P : (t + 1) * P].bitcast(FP8X4),
+                        scales=w1_scale[a][:, t * P : (t + 1) * P],
+                        in_=w1_bf[:, t * H : (t + 1) * H],
+                    )
+            for u in range(2):
+                for t in range(PACK):
+                    first_product(a, u, t)
+
+        nc.gpsimd.tensor_copy(
+            out=w2w[:].rearrange("p (t m b) -> p t m b", t=PACK, b=2),
+            in_=w2w_raw[:].rearrange("p (m t b) -> p t m b", t=PACK, b=2),
+        )
+        nc.gpsimd.tensor_copy(
+            out=w2s[:].rearrange("p (t m) -> p t m", t=PACK),
+            in_=w2s_raw[:].rearrange("p (m t) -> p t m", t=PACK),
+        )
+
+        g = [tile([P, S], F32, "g%d" % t) for t in range(PACK)]
+        th = [tile([P, PACK, SH], F32, "th%d" % u, tag="w1_raw%d" % u) for u in range(2)]
+        for u in range(2):
+            for t in range(PACK):
+                cols = slice(u * SH, (u + 1) * SH)
+                nc.vector.tensor_tensor(out=g[t][:, cols], in0=g_ps[u, t][:], in1=lot_sb[u, t][:], op=ALU.add)
+                nc.scalar.activation(out=th[u][:, t, :], in_=g[t][:, cols], func=ACT.Tanh)
+
+        w3_bf = tile([P, PACK * H], BF16, "w3_bf")
+        for u in range(2):
+            deal_columns(nc.scalar.copy, w3_bf, w3_raw[u], u * (P // 2), (u + 1) * (P // 2))
+
+        h = [tile([P, S], F32, "h%d" % t) for t in range(PACK)]
+        f_bf = {}
+
+        def weave_f(q):
+            f_bf[q] = tile([P, PACK * SQ], BF16, "f_bf%d" % q, tag="ring%d" % (q % 2))
+            nc.vector.tensor_tensor(
+                out=woven_by_lines(f_bf[q][:]),
+                in0=by_lines(th[q // 2][:, :, (q % 2) * SQ : (q % 2 + 1) * SQ]),
+                in1=rowvec["tgain"][:].unsqueeze(1).unsqueeze(3).broadcast_to([P, SQ // 4, PACK, 4]),
+                op=ALU.mult,
+            )
+
+        def second_product(q):
+            f_codes = tile([P, SQ], U32, "f_codes%d" % q)
+            f_scale = tile([P, SQ], U8, "f_scale%d" % q)
+            nc.vector.quantize_mx(out=f_codes[:].bitcast(FP8X4), scales=f_scale[:], in_=f_bf[q][:])
+            for pair in range(2):
+                h_ps = bank([P, 2, SQ], "h_ps%d%d" % (q, pair), 2 * q + pair)
+                for e in range(2):
+                    t = 2 * pair + e
+                    nc.tensor.matmul_mx(
+                        out=h_ps[:, e, :],
+                        lhsT=w2w[:, 2 * t * P : 2 * (t + 1) * P].bitcast(FP4X4),
+                        lhsT_scale=w2s[:, t * P : (t + 1) * P],
+                        rhs=f_codes[:].bitcast(FP8X4),
+                        rhs_scale=f_scale[:],
+                        start=True,
+                        stop=True,
+                    )
+                for e in range(2):
+                    nc.scalar.copy(out=h[2 * pair + e][:, q * SQ : (q + 1) * SQ], in_=h_ps[:, e, :])
+
+        weave_f(0)
+        for q in range(1, 4):
+            weave_f(q)
+            second_product(q - 1)
+        second_product(3)
+
+        w3_codes = tile([P, H], U32, "w3_codes")
+        w3_scale = tile([P, H], U8, "w3_scale")
+        y_codes = tile([P, M], U32, "y_codes")
+        y_scale = tile([P, M], U8, "y_scale")
+        out_rows = out_0.rearrange("(p t) m -> p t m", t=PACK)
+        out_words = out_1[0].rearrange("p m t -> p (m t)").bitcast(I32)
+        lcols = MH // LIST_ROWS
+        c, z_ps = [], []
+        for v in range(2):
+            c_v = tile([P, PACK, MH], F32, "c%d" % v, tag="ring%d" % v)
+            gained = tile([P, PACK, MH], F32, "gained%d" % v)
+            a_v = tile([P, PACK, MH], F32, "a%d" % v)
+            c.append(c_v)
+            for t in range(PACK):
+                nc.vector.tensor_copy(c_v[:, t, :], g[t][:].indirect(pos2_sb[:, v * lcols : (v + 1) * lcols]))
+            for t in range(PACK):
+                nc.scalar.activation(
+                    out=a_v[:, t, :],
+                    in_=h[t][:].indirect(pos1_sb[:, v * lcols : (v + 1) * lcols]),
+                    func=ACT.Sigmoid,
+                    bias=rowvec["thr"][:, t : t + 1],
+                    scale=rowvec["sharp"][:, t : t + 1],
+                )
+            for t in range(PACK):
+                gain = rowvec["mgain"][:, t : t + 1]
+                if v == 0:
+                    nc.vector.tensor_scalar(out=gained[:, t, :], in0=c_v[:, t, :], scalar1=gain, scalar2=None, op0=ALU.mult)
+                else:
+                    nc.scalar.activation(out=gained[:, t, :], in_=a_v[:, t, :], func=ACT.Copy, scale=gain)
+            if v == 0:
+                nc.vector.quantize_mx(out=w3_codes[:].bitcast(FP8X4), scales=w3_scale[:], in_=w3_bf[:])
+            d_bf = tile([P, PACK * MH], BF16, "d_bf%d" % v)
+            other = a_v if v == 0 else c_v
+            nc.vector.tensor_tensor(out=woven_by_lines(d_bf[:]), in0=by_lines(other[:]), in1=by_lines(gained[:]), op=ALU.mult)
+            d_codes = tile([P, MH], U32, "d_codes%d" % v)
+            d_scale = tile([P, MH], U8, "d_scale%d" % v)
+            nc.vector.quantize_mx(out=d_codes[:].bitcast(FP8X4), scales=d_scale[:], in_=d_bf[:])
+            for e in range(2):
+                z_ps.append(bank([P, PACK, MQ], "z_ps%d%d" % (v, e), 2 * v + e))
+                for t in range(PACK):
+                    nc.tensor.matmul_mx(
+                        out=z_ps[-1][:, t, :],
+                        lhsT=w3_codes[:, t * P : (t + 1) * P].bitcast(FP8X4),
+                        lhsT_scale=w3_scale[:, t * P : (t + 1) * P],
+                        rhs=d_codes[:, e * MQ : (e + 1) * MQ].bitcast(FP8X4),
+                        rhs_scale=d_scale[:, e * MQ : (e + 1) * MQ],
+                        start=True,
+                        stop=True,
+                    )
+
+        for first, last in ((0, 2), (2, 3), (3, 4)):
+            width = (last - first) * MQ
+            cols = slice(first * MQ, last * MQ)
+            z = tile([P, PACK, width], F32, "z%d" % first)
+            y = tile([P, PACK, width], F32, "y%d" % first)
+            for i in range(first, last):
+                nc.vector.tensor_tensor(
+                    out=z[:, :, (i - first) * MQ : (i - first + 1) * MQ],
+                    in0=z_ps[i][:],
+                    in1=c[i // 2][:, :, (i % 2) * MQ : (i % 2 + 1) * MQ],
+                    op=ALU.max,
+                )
+            for t in range(PACK):
+                nc.scalar.activation(out=y[:, t, :], in_=z[:, t, :], func=ACT.Copy, scale=rowvec["ygain"][:, t : t + 1])
+            nc.sync.dma_start(out=out_rows[:, :, cols], in_=y[:])
+            y_bf = tile([P, PACK * width], BF16, "y_bf%d" % first)
+            weave = nc.scalar.copy if first == 0 else nc.vector.tensor_copy
+            weave(out=woven_by_lines(y_bf[:]), in_=by_lines(y[:]))
+            nc.vector.quantize_mx(out=y_codes[:, cols].bitcast(FP8X4), scales=y_scale[:, cols], in_=y_bf[:])
+            if last != 3:
+                done = slice((last - 2) * MQ, last * MQ)
+                nc.sync.dma_start(out=out_words[:, done], in_=y_codes[:, done].bitcast(I32))
+        for q in range(4):
+            queue = nc.sync if q % 2 else nc.scalar
+            queue.dma_start(
+                out=out_2[0, 4 * q : 4 * q + 4, :].bitcast(I32),
+                in_=y_scale[32 * q : 32 * q + 4, :].bitcast(I32),
+            )

@@ -25,6 +25,7 @@ SQ = S // 4
 MH = M // 2
 MQ = M // 4
 LIST_ROWS = 16
+SCALAR_SHARE = 44
 
 
 def tile_list_gelcard_reaction_features_kernel(
@@ -44,7 +45,7 @@ def tile_list_gelcard_reaction_features_kernel(
 
         def deal_columns(engine_copy, grouped, raw, m0, m1):
             out = grouped[:].rearrange("p (t m j) -> p m j t", t=PACK, j=PACK)[:, m0:m1]
-            engine_copy(out=out, in_=raw[:].rearrange("p j (m t) -> p m j t", t=PACK))
+            engine_copy(out=out, in_=raw[:].rearrange("p j (m t) -> p m j t", t=PACK)[:, m0:m1])
 
         def by_lines(planes):
             return planes.rearrange("p t (c i) -> p c t i", i=4)
@@ -59,11 +60,10 @@ def tile_list_gelcard_reaction_features_kernel(
         w2w_raw = tile([P, 2 * H], U8, "w2w_raw")
         w2s_raw = tile([P, H], U8, "w2s_raw")
         nc.vector.memset(tscale[:].bitcast(I32), 0)
-        nc.gpsimd.memset(w2s_raw[:].bitcast(I32), 0)
+        nc.vector.memset(w2s_raw[:].bitcast(I32), 0)
         twords = [tile([P, T], U32, "twords%d" % a) for a in range(PASSES)]
         w1_rows = w1.rearrange("(a p j) c -> a p j c", p=P, j=PACK)
-        w1_raw = [tile([P, PACK, H], F32, "w1_raw%d" % a) for a in range(PASSES - 1)]
-        w1_last = [tile([P, PACK, H // 2], F32, "w1_last%d" % u) for u in range(2)]
+        w1_raw = [tile([P, PACK, H], F32, "w1_raw%d" % a) for a in range(PASSES)]
         rowvec = {}
 
         def load_rowvec(name, vec):
@@ -86,6 +86,7 @@ def tile_list_gelcard_reaction_features_kernel(
             )
         nc.sync.dma_start(pos2_sb[:], pos2)
         nc.sync.dma_start(pos1_sb[:], pos1)
+        nc.sync.dma_start(out=w1_raw[1][:], in_=w1_rows[1])
         load_table(1)
         nc.sync.dma_start(out=w2w_raw[:].bitcast(I32), in_=w2_words[0].bitcast(I32))
         for q in range(4):
@@ -93,29 +94,22 @@ def tile_list_gelcard_reaction_features_kernel(
                 out=w2s_raw[32 * q : 32 * q + 4, :].bitcast(I32),
                 in_=w2_scales[0, 4 * q : 4 * q + 4, :].bitcast(I32),
             )
-        nc.sync.dma_start(out=w1_raw[1][:], in_=w1_rows[1])
         load_table(2)
-        for u in range(2):
-            nc.sync.dma_start(out=w1_last[u][:], in_=w1_rows[PASSES - 1][:, :, u * (H // 2) : (u + 1) * (H // 2)])
+        nc.sync.dma_start(out=w1_raw[2][:], in_=w1_rows[2])
         lot_rows = lot.rearrange("(p t) s -> p t s", t=PACK)
-        lot_sb = {}
-        for u in range(2):
-            for t in range(PACK):
-                lot_sb[u, t] = tile([P, SH], F32, "lot%d%d" % (u, t))
-                nc.sync.dma_start(out=lot_sb[u, t][:], in_=lot_rows[:, t, u * SH : (u + 1) * SH])
-            if u == 0:
-                load_rowvec("tgain", tgain)
-        w3_rows = w3.rearrange("(p j) c -> p j c", j=PACK)
-        w3_raw = [tile([P, PACK, H // 2], F32, "w3_raw%d" % u) for u in range(2)]
-        for u in range(2):
-            nc.sync.dma_start(out=w3_raw[u][:], in_=w3_rows[:, :, u * (H // 2) : (u + 1) * (H // 2)])
+        lot_sb = [tile([P, S], F32, "lot%d" % t) for t in range(PACK)]
+        for t in range(PACK):
+            nc.sync.dma_start(out=lot_sb[t][:], in_=lot_rows[:, t, :])
+        load_rowvec("tgain", tgain)
+        w3_raw = tile([P, PACK, H], F32, "w3_raw")
+        nc.sync.dma_start(out=w3_raw[:], in_=w3.rearrange("(p j) c -> p j c", j=PACK))
         for name, vec in (("mgain", mgain), ("sharp", sharp), ("thr", thr), ("ygain", ygain)):
             load_rowvec(name, vec)
 
         vscale = tile([P, S], U8, "vscale")
         nc.vector.tensor_copy(vscale[:], tscale[:].indirect(offs_sb[:]))
         vwords = [tile([P, S], U32, "vwords%d" % a) for a in range(PASSES)]
-        w1_codes = [tile([P, H], U32, "w1_codes%d" % a) for a in range(PASSES)]
+        w1_codes = [tile([P, H], U32, "w1_codes%d" % a, tag="tscale" if a == 0 else "") for a in range(PASSES)]
         w1_scale = [tile([P, H], U8, "w1_scale%d" % a) for a in range(PASSES)]
         w2w = tile([P, 2 * H], U8, "w2w")
         w2s = tile([P, H], U8, "w2s")
@@ -135,42 +129,41 @@ def tile_list_gelcard_reaction_features_kernel(
         for a in range(PASSES):
             nc.vector.tensor_copy(vwords[a][:], twords[a][:].indirect(offs_sb[:]))
             w1_bf = tile([P, PACK * H], BF16, "w1_bf%d" % a)
-            if a < PASSES - 1:
+            if a == 0:
                 deal_columns(nc.scalar.copy, w1_bf, w1_raw[a], 0, P)
-                nc.vector.quantize_mx(out=w1_codes[a][:].bitcast(FP8X4), scales=w1_scale[a][:], in_=w1_bf[:])
             else:
-                deal_columns(nc.scalar.copy, w1_bf, w1_last[0], 0, P // 2)
-                deal_columns(nc.vector.tensor_copy, w1_bf, w1_last[1], P // 2, P)
-                for t in range(PACK):
-                    nc.vector.quantize_mx(
-                        out=w1_codes[a][:, t * P : (t + 1) * P].bitcast(FP8X4),
-                        scales=w1_scale[a][:, t * P : (t + 1) * P],
-                        in_=w1_bf[:, t * H : (t + 1) * H],
-                    )
-            for u in range(2):
-                for t in range(PACK):
+                deal_columns(nc.scalar.copy, w1_bf, w1_raw[a], 0, SCALAR_SHARE)
+                deal_columns(nc.vector.tensor_copy, w1_bf, w1_raw[a], SCALAR_SHARE, P)
+            step = H if a < PASSES - 1 else P
+            for c0 in range(0, H, step):
+                nc.vector.quantize_mx(
+                    out=w1_codes[a][:, c0 : c0 + step].bitcast(FP8X4),
+                    scales=w1_scale[a][:, c0 : c0 + step],
+                    in_=w1_bf[:, PACK * c0 : PACK * (c0 + step)],
+                )
+            if a == 1:
+                nc.scalar.copy(
+                    out=w2w[:].bitcast(U16).rearrange("p (t m) -> p m t", t=PACK),
+                    in_=w2w_raw[:].bitcast(U16).rearrange("p (m t) -> p m t", t=PACK),
+                )
+                nc.vector.tensor_copy(
+                    out=w2s[:].rearrange("p (t m) -> p m t", t=PACK),
+                    in_=w2s_raw[:].rearrange("p (m t) -> p m t", t=PACK),
+                )
+            for t in range(PACK):
+                for u in range(2):
                     first_product(a, u, t)
-
-        nc.gpsimd.tensor_copy(
-            out=w2w[:].rearrange("p (t m b) -> p t m b", t=PACK, b=2),
-            in_=w2w_raw[:].rearrange("p (m t b) -> p t m b", t=PACK, b=2),
-        )
-        nc.gpsimd.tensor_copy(
-            out=w2s[:].rearrange("p (t m) -> p t m", t=PACK),
-            in_=w2s_raw[:].rearrange("p (m t) -> p t m", t=PACK),
-        )
 
         g = [tile([P, S], F32, "g%d" % t) for t in range(PACK)]
         th = [tile([P, PACK, SH], F32, "th%d" % u, tag="w1_raw%d" % u) for u in range(2)]
-        for u in range(2):
-            for t in range(PACK):
+        for t in range(PACK):
+            for u in range(2):
                 cols = slice(u * SH, (u + 1) * SH)
-                nc.vector.tensor_tensor(out=g[t][:, cols], in0=g_ps[u, t][:], in1=lot_sb[u, t][:], op=ALU.add)
+                nc.vector.tensor_tensor(out=g[t][:, cols], in0=g_ps[u, t][:], in1=lot_sb[t][:, cols], op=ALU.add)
                 nc.scalar.activation(out=th[u][:, t, :], in_=g[t][:, cols], func=ACT.Tanh)
 
         w3_bf = tile([P, PACK * H], BF16, "w3_bf")
-        for u in range(2):
-            deal_columns(nc.scalar.copy, w3_bf, w3_raw[u], u * (P // 2), (u + 1) * (P // 2))
+        deal_columns(nc.scalar.copy, w3_bf, w3_raw, 0, P)
 
         h = [tile([P, S], F32, "h%d" % t) for t in range(PACK)]
         f_bf = {}

@@ -61,6 +61,9 @@ def tile_list_gelcard_reaction_features_kernel(
         w2s_raw = tile([P, H], U8, "w2s_raw")
         nc.vector.memset(tscale[:].bitcast(I32), 0)
         nc.vector.memset(w2s_raw[:].bitcast(I32), 0)
+        warm = tile([P, 2], F32, "warm")
+        nc.gpsimd.memset(warm[:, 0:1], 0.0)
+        nc.scalar.activation(out=warm[:, 1:2], in_=warm[:, 0:1], func=ACT.Sigmoid)
         twords = [tile([P, T], U32, "twords%d" % a) for a in range(PASSES)]
         w1_rows = w1.rearrange("(a p j) c -> a p j c", p=P, j=PACK)
         w1_raw = [tile([P, PACK, H], F32, "w1_raw%d" % a) for a in range(PASSES)]

@@ -19,13 +19,15 @@ ACT = mybir.ActivationFunctionType
 P = 128
 PACK = 4
 PASSES = K // (P * PACK)
-BANK = 512
-SH = S // 2
-SQ = S // 4
-MH = M // 2
-MQ = M // 4
-LIST_ROWS = 16
-SCALAR_SHARE = 44
+QUADS, QUAD = 4, 32
+SCALE_ROWS = 4
+LINE = 4
+S_HALF = S // 2
+S_QUARTER = S // 4
+M_HALF = M // 2
+M_QUARTER = M // 4
+PER_COLUMN = 16
+SCALAR_SHARE = (128, 96, 44)
 
 
 def tile_list_gelcard_reaction_features_kernel(
@@ -43,19 +45,21 @@ def tile_list_gelcard_reaction_features_kernel(
         def bank(shape, name, index):
             return ps.tile(shape, F32, name=name, tag="bank%d" % index)
 
-        def deal_columns(engine_copy, grouped, raw, m0, m1):
-            out = grouped[:].rearrange("p (t m j) -> p m j t", t=PACK, j=PACK)[:, m0:m1]
-            engine_copy(out=out, in_=raw[:].rearrange("p j (m t) -> p m j t", t=PACK)[:, m0:m1])
+        def deal_and_round(copy, dealt, raw, m0, m1):
+            copy(
+                out=dealt[:].rearrange("p (t m j) -> p m j t", t=PACK, j=PACK)[:, m0:m1],
+                in_=raw[:].rearrange("p j (m t) -> p m j t", t=PACK)[:, m0:m1],
+            )
 
-        def by_lines(planes):
-            return planes.rearrange("p t (c i) -> p c t i", i=4)
+        def planes_walk(planes):
+            return planes.rearrange("p t (c i) -> p c t i", i=LINE)
 
-        def woven_by_lines(woven):
-            return woven.rearrange("p (c i t) -> p c t i", i=4, t=PACK)
+        def woven_walk(woven):
+            return woven.rearrange("p (c i t) -> p c t i", i=LINE, t=PACK)
 
-        offs_sb = tile([P, S // LIST_ROWS], U16, "offs_sb")
-        pos1_sb = tile([P, M // LIST_ROWS], U16, "pos1_sb")
-        pos2_sb = tile([P, M // LIST_ROWS], U16, "pos2_sb")
+        offs_sb = tile([P, S // PER_COLUMN], U16, "offs_sb")
+        pos1_sb = tile([P, M // PER_COLUMN], U16, "pos1_sb")
+        pos2_sb = tile([P, M // PER_COLUMN], U16, "pos2_sb")
         tscale = tile([P, T], U8, "tscale")
         w2w_raw = tile([P, 2 * H], U8, "w2w_raw")
         w2s_raw = tile([P, H], U8, "w2s_raw")
@@ -82,23 +86,23 @@ def tile_list_gelcard_reaction_features_kernel(
         nc.sync.dma_start(offs_sb[:], offs)
         load_table(0)
         nc.sync.dma_start(out=w1_raw[0][:], in_=w1_rows[0])
-        for q in range(4):
+        for q in range(QUADS):
             nc.sync.dma_start(
-                out=tscale[32 * q : 32 * q + 4 * PASSES, :].bitcast(I32),
-                in_=tab_scales[:, 4 * q : 4 * q + 4, :].bitcast(I32),
+                out=tscale[QUAD * q : QUAD * q + SCALE_ROWS * PASSES, :].bitcast(I32),
+                in_=tab_scales[:, SCALE_ROWS * q : SCALE_ROWS * (q + 1), :].bitcast(I32),
             )
         nc.sync.dma_start(pos2_sb[:], pos2)
         nc.sync.dma_start(pos1_sb[:], pos1)
         nc.sync.dma_start(out=w1_raw[1][:], in_=w1_rows[1])
         load_table(1)
-        nc.sync.dma_start(out=w2w_raw[:].bitcast(I32), in_=w2_words[0].bitcast(I32))
-        for q in range(4):
-            nc.sync.dma_start(
-                out=w2s_raw[32 * q : 32 * q + 4, :].bitcast(I32),
-                in_=w2_scales[0, 4 * q : 4 * q + 4, :].bitcast(I32),
-            )
         load_table(2)
         nc.sync.dma_start(out=w1_raw[2][:], in_=w1_rows[2])
+        nc.sync.dma_start(out=w2w_raw[:].bitcast(I32), in_=w2_words[0].bitcast(I32))
+        for q in range(QUADS):
+            nc.sync.dma_start(
+                out=w2s_raw[QUAD * q : QUAD * q + SCALE_ROWS, :].bitcast(I32),
+                in_=w2_scales[0, SCALE_ROWS * q : SCALE_ROWS * (q + 1), :].bitcast(I32),
+            )
         lot_rows = lot.rearrange("(p t) s -> p t s", t=PACK)
         lot_sb = [tile([P, S], F32, "lot%d" % t) for t in range(PACK)]
         for t in range(PACK):
@@ -111,81 +115,99 @@ def tile_list_gelcard_reaction_features_kernel(
 
         vscale = tile([P, S], U8, "vscale")
         nc.vector.tensor_copy(vscale[:], tscale[:].indirect(offs_sb[:]))
-        vwords = [tile([P, S], U32, "vwords%d" % a) for a in range(PASSES)]
+        vwords = {0: tile([P, S], U32, "vwords0")}
         w1_codes = [tile([P, H], U32, "w1_codes%d" % a, tag="tscale" if a == 0 else "") for a in range(PASSES)]
         w1_scale = [tile([P, H], U8, "w1_scale%d" % a) for a in range(PASSES)]
-        w2w = tile([P, 2 * H], U8, "w2w")
-        w2s = tile([P, H], U8, "w2s")
-        g_ps = {(u, t): bank([P, BANK], "g_ps%d%d" % (u, t), PACK * u + t) for u in range(2) for t in range(PACK)}
+        g_ps = {(u, t): bank([P, S_HALF], "g_ps%d%d" % (u, t), PACK * u + t) for u in range(2) for t in range(PACK)}
 
         def first_product(a, u, t):
             nc.tensor.matmul_mx(
                 out=g_ps[u, t][:],
                 lhsT=w1_codes[a][:, t * P : (t + 1) * P].bitcast(FP8X4),
                 lhsT_scale=w1_scale[a][:, t * P : (t + 1) * P],
-                rhs=vwords[a][:, u * SH : (u + 1) * SH].bitcast(FP8X4),
-                rhs_scale=vscale[4 * a : P, u * SH : (u + 1) * SH],
+                rhs=vwords[a][:, u * S_HALF : (u + 1) * S_HALF].bitcast(FP8X4),
+                rhs_scale=vscale[SCALE_ROWS * a : P, u * S_HALF : (u + 1) * S_HALF],
                 start=(a == 0),
                 stop=(a == PASSES - 1),
             )
 
-        for a in range(PASSES):
-            nc.vector.tensor_copy(vwords[a][:], twords[a][:].indirect(offs_sb[:]))
-            w1_bf = tile([P, PACK * H], BF16, "w1_bf%d" % a)
-            if a == 0:
-                deal_columns(nc.scalar.copy, w1_bf, w1_raw[a], 0, P)
-            else:
-                deal_columns(nc.scalar.copy, w1_bf, w1_raw[a], 0, SCALAR_SHARE)
-                deal_columns(nc.vector.tensor_copy, w1_bf, w1_raw[a], SCALAR_SHARE, P)
-            step = H if a < PASSES - 1 else P
-            for c0 in range(0, H, step):
-                nc.vector.quantize_mx(
-                    out=w1_codes[a][:, c0 : c0 + step].bitcast(FP8X4),
-                    scales=w1_scale[a][:, c0 : c0 + step],
-                    in_=w1_bf[:, PACK * c0 : PACK * (c0 + step)],
-                )
-            if a == 1:
-                nc.scalar.copy(
-                    out=w2w[:].bitcast(U16).rearrange("p (t m) -> p m t", t=PACK),
-                    in_=w2w_raw[:].bitcast(U16).rearrange("p (m t) -> p m t", t=PACK),
-                )
-                nc.vector.tensor_copy(
-                    out=w2s[:].rearrange("p (t m) -> p m t", t=PACK),
-                    in_=w2s_raw[:].rearrange("p (m t) -> p m t", t=PACK),
-                )
-            for t in range(PACK):
-                for u in range(2):
-                    first_product(a, u, t)
+        def pick_table(a, width):
+            for c0 in range(0, S, width):
+                entries = offs_sb[:, c0 // PER_COLUMN : (c0 + width) // PER_COLUMN]
+                nc.vector.tensor_copy(vwords[a][:, c0 : c0 + width], twords[a][:].indirect(entries))
 
-        g = [tile([P, S], F32, "g%d" % t) for t in range(PACK)]
-        th = [tile([P, PACK, SH], F32, "th%d" % u, tag="w1_raw%d" % u) for u in range(2)]
+        def quantize_w1(a, width):
+            w1_bf = tile([P, PACK * H], BF16, "w1_bf%d" % a)
+            share = SCALAR_SHARE[a]
+            deal_and_round(nc.scalar.copy, w1_bf, w1_raw[a], 0, share)
+            if share < P:
+                deal_and_round(nc.vector.tensor_copy, w1_bf, w1_raw[a], share, P)
+            for c0 in range(0, H, width):
+                nc.vector.quantize_mx(
+                    out=w1_codes[a][:, c0 : c0 + width].bitcast(FP8X4),
+                    scales=w1_scale[a][:, c0 : c0 + width],
+                    in_=w1_bf[:, PACK * c0 : PACK * (c0 + width)],
+                )
+
+        pick_table(0, S)
+        quantize_w1(0, H)
+        for u in range(2):
+            for t in range(PACK):
+                first_product(0, u, t)
+        quantize_w1(1, H)
+        vwords[1] = tile([P, S], U32, "vwords1", tag="w1_bf1")
+        pick_table(1, S_HALF)
+        for u in range(2):
+            for t in range(PACK):
+                first_product(1, u, t)
+        vwords[2] = tile([P, S], U32, "vwords2")
+        pick_table(2, S)
+        quantize_w1(2, P)
         for t in range(PACK):
             for u in range(2):
-                cols = slice(u * SH, (u + 1) * SH)
+                first_product(2, u, t)
+
+        w2w = tile([P, 2 * H], U8, "w2w")
+        w2s = tile([P, H], U8, "w2s", tag="w1_bf2")
+        nc.scalar.copy(
+            out=w2w[:].bitcast(U16).rearrange("p (t m) -> p m t", t=PACK),
+            in_=w2w_raw[:].bitcast(U16).rearrange("p (m t) -> p m t", t=PACK),
+        )
+        nc.vector.tensor_copy(
+            out=w2s[:].rearrange("p (t m) -> p m t", t=PACK),
+            in_=w2s_raw[:].rearrange("p (m t) -> p m t", t=PACK),
+        )
+
+        g = [tile([P, S], F32, "g%d" % t) for t in range(PACK)]
+        tanh_g = [tile([P, PACK, S_HALF], F32, "tanh_g%d" % u, tag="w1_raw%d" % u) for u in range(2)]
+        for t in range(PACK):
+            for u in range(2):
+                cols = slice(u * S_HALF, (u + 1) * S_HALF)
                 nc.vector.tensor_tensor(out=g[t][:, cols], in0=g_ps[u, t][:], in1=lot_sb[t][:, cols], op=ALU.add)
-                nc.scalar.activation(out=th[u][:, t, :], in_=g[t][:, cols], func=ACT.Tanh)
+                nc.scalar.activation(out=tanh_g[u][:, t, :], in_=g[t][:, cols], func=ACT.Tanh)
 
         w3_bf = tile([P, PACK * H], BF16, "w3_bf")
-        deal_columns(nc.scalar.copy, w3_bf, w3_raw, 0, P)
+        deal_and_round(nc.scalar.copy, w3_bf, w3_raw, 0, P)
 
         h = [tile([P, S], F32, "h%d" % t) for t in range(PACK)]
         f_bf = {}
 
-        def weave_f(q):
-            f_bf[q] = tile([P, PACK * SQ], BF16, "f_bf%d" % q, tag="ring%d" % (q % 2))
+        def weave_f(quarter):
+            f_bf[quarter] = tile([P, PACK * S_QUARTER], BF16, "f_bf%d" % quarter, tag="ring%d" % (quarter % 2))
+            c0 = (quarter % 2) * S_QUARTER
             nc.vector.tensor_tensor(
-                out=woven_by_lines(f_bf[q][:]),
-                in0=by_lines(th[q // 2][:, :, (q % 2) * SQ : (q % 2 + 1) * SQ]),
-                in1=rowvec["tgain"][:].unsqueeze(1).unsqueeze(3).broadcast_to([P, SQ // 4, PACK, 4]),
+                out=woven_walk(f_bf[quarter][:]),
+                in0=planes_walk(tanh_g[quarter // 2][:, :, c0 : c0 + S_QUARTER]),
+                in1=rowvec["tgain"][:].unsqueeze(1).unsqueeze(3).broadcast_to([P, S_QUARTER // LINE, PACK, LINE]),
                 op=ALU.mult,
             )
 
-        def second_product(q):
-            f_codes = tile([P, SQ], U32, "f_codes%d" % q)
-            f_scale = tile([P, SQ], U8, "f_scale%d" % q)
-            nc.vector.quantize_mx(out=f_codes[:].bitcast(FP8X4), scales=f_scale[:], in_=f_bf[q][:])
+        def second_product(quarter):
+            f_codes = tile([P, S_QUARTER], U32, "f_codes%d" % quarter)
+            f_scale = tile([P, S_QUARTER], U8, "f_scale%d" % quarter)
+            nc.vector.quantize_mx(out=f_codes[:].bitcast(FP8X4), scales=f_scale[:], in_=f_bf[quarter][:])
             for pair in range(2):
-                h_ps = bank([P, 2, SQ], "h_ps%d%d" % (q, pair), 2 * q + pair)
+                h_ps = bank([P, 2, S_QUARTER], "h_ps%d%d" % (quarter, pair), 2 * quarter + pair)
                 for e in range(2):
                     t = 2 * pair + e
                     nc.tensor.matmul_mx(
@@ -198,12 +220,14 @@ def tile_list_gelcard_reaction_features_kernel(
                         stop=True,
                     )
                 for e in range(2):
-                    nc.scalar.copy(out=h[2 * pair + e][:, q * SQ : (q + 1) * SQ], in_=h_ps[:, e, :])
+                    nc.scalar.copy(
+                        out=h[2 * pair + e][:, quarter * S_QUARTER : (quarter + 1) * S_QUARTER], in_=h_ps[:, e, :]
+                    )
 
         weave_f(0)
-        for q in range(1, 4):
-            weave_f(q)
-            second_product(q - 1)
+        for quarter in range(1, 4):
+            weave_f(quarter)
+            second_product(quarter - 1)
         second_product(3)
 
         w3_codes = tile([P, H], U32, "w3_codes")
@@ -212,75 +236,104 @@ def tile_list_gelcard_reaction_features_kernel(
         y_scale = tile([P, M], U8, "y_scale")
         out_rows = out_0.rearrange("(p t) m -> p t m", t=PACK)
         out_words = out_1[0].rearrange("p m t -> p (m t)").bitcast(I32)
-        lcols = MH // LIST_ROWS
-        c, z_ps = [], []
-        for v in range(2):
-            c_v = tile([P, PACK, MH], F32, "c%d" % v, tag="ring%d" % v)
-            gained = tile([P, PACK, MH], F32, "gained%d" % v)
-            a_v = tile([P, PACK, MH], F32, "a%d" % v)
-            c.append(c_v)
+        control, z_ps, z = [], [], {}
+        pieces = ((0, 2), (2, 3), (3, 4))
+
+        def take_max(first, last):
+            z[first] = tile([P, PACK, (last - first) * M_QUARTER], F32, "z%d" % first)
+            for i in range(first, last):
+                nc.vector.tensor_tensor(
+                    out=z[first][:, :, (i - first) * M_QUARTER : (i - first + 1) * M_QUARTER],
+                    in0=z_ps[i][:],
+                    in1=control[i // 2][:, :, (i % 2) * M_QUARTER : (i % 2 + 1) * M_QUARTER],
+                    op=ALU.max,
+                )
+
+        def pick_and_look(v):
+            entries = slice(v * M_HALF // PER_COLUMN, (v + 1) * M_HALF // PER_COLUMN)
+            control.append(tile([P, PACK, M_HALF], F32, "control%d" % v, tag="ring%d" % v))
+            gained = tile([P, PACK, M_HALF], F32, "gained%d" % v)
+            gate = tile([P, PACK, M_HALF], F32, "gate%d" % v)
             for t in range(PACK):
-                nc.vector.tensor_copy(c_v[:, t, :], g[t][:].indirect(pos2_sb[:, v * lcols : (v + 1) * lcols]))
+                nc.vector.tensor_copy(control[v][:, t, :], g[t][:].indirect(pos2_sb[:, entries]))
             for t in range(PACK):
                 nc.scalar.activation(
-                    out=a_v[:, t, :],
-                    in_=h[t][:].indirect(pos1_sb[:, v * lcols : (v + 1) * lcols]),
+                    out=gate[:, t, :],
+                    in_=h[t][:].indirect(pos1_sb[:, entries]),
                     func=ACT.Sigmoid,
                     bias=rowvec["thr"][:, t : t + 1],
                     scale=rowvec["sharp"][:, t : t + 1],
                 )
-            for t in range(PACK):
-                gain = rowvec["mgain"][:, t : t + 1]
-                if v == 0:
-                    nc.vector.tensor_scalar(out=gained[:, t, :], in0=c_v[:, t, :], scalar1=gain, scalar2=None, op0=ALU.mult)
-                else:
-                    nc.scalar.activation(out=gained[:, t, :], in_=a_v[:, t, :], func=ACT.Copy, scale=gain)
-            if v == 0:
-                nc.vector.quantize_mx(out=w3_codes[:].bitcast(FP8X4), scales=w3_scale[:], in_=w3_bf[:])
-            d_bf = tile([P, PACK * MH], BF16, "d_bf%d" % v)
-            other = a_v if v == 0 else c_v
-            nc.vector.tensor_tensor(out=woven_by_lines(d_bf[:]), in0=by_lines(other[:]), in1=by_lines(gained[:]), op=ALU.mult)
-            d_codes = tile([P, MH], U32, "d_codes%d" % v)
-            d_scale = tile([P, MH], U8, "d_scale%d" % v)
-            nc.vector.quantize_mx(out=d_codes[:].bitcast(FP8X4), scales=d_scale[:], in_=d_bf[:])
+            return gate, gained
+
+        def third_product(v, plain, gained, width, tag):
+            d_bf = tile([P, PACK * M_HALF], BF16, "d_bf%d" % v, tag=tag)
+            d_codes = tile([P, M_HALF], U32, "d_codes%d" % v)
+            d_scale = tile([P, M_HALF], U8, "d_scale%d" % v)
+            for m0 in range(0, M_HALF, width):
+                nc.vector.tensor_tensor(
+                    out=woven_walk(d_bf[:, PACK * m0 : PACK * (m0 + width)]),
+                    in0=planes_walk(plain[:, :, m0 : m0 + width]),
+                    in1=planes_walk(gained[:, :, m0 : m0 + width]),
+                    op=ALU.mult,
+                )
+            for m0 in range(0, M_HALF, width):
+                nc.vector.quantize_mx(
+                    out=d_codes[:, m0 : m0 + width].bitcast(FP8X4),
+                    scales=d_scale[:, m0 : m0 + width],
+                    in_=d_bf[:, PACK * m0 : PACK * (m0 + width)],
+                )
             for e in range(2):
-                z_ps.append(bank([P, PACK, MQ], "z_ps%d%d" % (v, e), 2 * v + e))
+                z_ps.append(bank([P, PACK, M_QUARTER], "z_ps%d%d" % (v, e), 2 * v + e))
                 for t in range(PACK):
                     nc.tensor.matmul_mx(
                         out=z_ps[-1][:, t, :],
                         lhsT=w3_codes[:, t * P : (t + 1) * P].bitcast(FP8X4),
                         lhsT_scale=w3_scale[:, t * P : (t + 1) * P],
-                        rhs=d_codes[:, e * MQ : (e + 1) * MQ].bitcast(FP8X4),
-                        rhs_scale=d_scale[:, e * MQ : (e + 1) * MQ],
+                        rhs=d_codes[:, e * M_QUARTER : (e + 1) * M_QUARTER].bitcast(FP8X4),
+                        rhs_scale=d_scale[:, e * M_QUARTER : (e + 1) * M_QUARTER],
                         start=True,
                         stop=True,
                     )
 
-        for first, last in ((0, 2), (2, 3), (3, 4)):
-            width = (last - first) * MQ
-            cols = slice(first * MQ, last * MQ)
-            z = tile([P, PACK, width], F32, "z%d" % first)
+        gate, gained = pick_and_look(0)
+        for t in range(PACK):
+            nc.vector.tensor_scalar(
+                out=gained[:, t, :], in0=control[0][:, t, :], scalar1=rowvec["mgain"][:, t : t + 1], scalar2=None,
+                op0=ALU.mult,
+            )
+        nc.vector.quantize_mx(out=w3_codes[:].bitcast(FP8X4), scales=w3_scale[:], in_=w3_bf[:])
+        third_product(0, gate, gained, M_HALF, "d_bf0")
+
+        gate, gained = pick_and_look(1)
+        for t in range(PACK):
+            nc.scalar.activation(
+                out=gained[:, t, :], in_=gate[:, t, :], func=ACT.Copy, scale=rowvec["mgain"][:, t : t + 1]
+            )
+        take_max(*pieces[0])
+        third_product(1, control[1], gained, M_QUARTER, "ring0")
+        for first, last in pieces[1:]:
+            take_max(first, last)
+
+        for first, last in pieces:
+            width = (last - first) * M_QUARTER
+            cols = slice(first * M_QUARTER, last * M_QUARTER)
             y = tile([P, PACK, width], F32, "y%d" % first)
-            for i in range(first, last):
-                nc.vector.tensor_tensor(
-                    out=z[:, :, (i - first) * MQ : (i - first + 1) * MQ],
-                    in0=z_ps[i][:],
-                    in1=c[i // 2][:, :, (i % 2) * MQ : (i % 2 + 1) * MQ],
-                    op=ALU.max,
-                )
             for t in range(PACK):
-                nc.scalar.activation(out=y[:, t, :], in_=z[:, t, :], func=ACT.Copy, scale=rowvec["ygain"][:, t : t + 1])
+                nc.scalar.activation(
+                    out=y[:, t, :], in_=z[first][:, t, :], func=ACT.Copy, scale=rowvec["ygain"][:, t : t + 1]
+                )
             nc.sync.dma_start(out=out_rows[:, :, cols], in_=y[:])
             y_bf = tile([P, PACK * width], BF16, "y_bf%d" % first)
             weave = nc.scalar.copy if first == 0 else nc.vector.tensor_copy
-            weave(out=woven_by_lines(y_bf[:]), in_=by_lines(y[:]))
+            weave(out=woven_walk(y_bf[:]), in_=planes_walk(y[:]))
             nc.vector.quantize_mx(out=y_codes[:, cols].bitcast(FP8X4), scales=y_scale[:, cols], in_=y_bf[:])
-            if last != 3:
-                done = slice((last - 2) * MQ, last * MQ)
-                nc.sync.dma_start(out=out_words[:, done], in_=y_codes[:, done].bitcast(I32))
-        for q in range(4):
+            if last % 2 == 0:
+                half = slice(last * M_QUARTER - M_HALF, last * M_QUARTER)
+                nc.sync.dma_start(out=out_words[:, half], in_=y_codes[:, half].bitcast(I32))
+        for q in range(QUADS):
             queue = nc.sync if q % 2 else nc.scalar
             queue.dma_start(
-                out=out_2[0, 4 * q : 4 * q + 4, :].bitcast(I32),
-                in_=y_scale[32 * q : 32 * q + 4, :].bitcast(I32),
+                out=out_2[0, SCALE_ROWS * q : SCALE_ROWS * (q + 1), :].bitcast(I32),
+                in_=y_scale[QUAD * q : QUAD * q + SCALE_ROWS, :].bitcast(I32),
             )

from contextlib import ExitStack

import concourse.mybir as mybir

K, T, H, S, M = 1536, 2048, 512, 1024, 512
FLOPS = 2 * (K * H * S + H * H * S + H * H * M)

F32 = mybir.dt.float32
BF16 = mybir.dt.bfloat16
I32 = mybir.dt.int32
U32 = mybir.dt.uint32
U16 = mybir.dt.uint16
U8 = mybir.dt.uint8
FP8X4 = mybir.dt.float8_e4m3fn_x4
FP4X4 = mybir.dt.float4_e2m1fn_x4
ALU = mybir.AluOpType
ACT = mybir.ActivationFunctionType

P = 128
PACK = 4
PASSES = K // (P * PACK)
QUADS, QUAD = 4, 32
SCALE_ROWS = 4
LINE = 4
S_HALF = S // 2
S_QUARTER = S // 4
M_HALF = M // 2
M_QUARTER = M // 4
PER_COLUMN = 16
SCALAR_SHARE = (128, 96, 44)


def tile_list_gelcard_reaction_features_kernel(
    tc, tab_words, tab_scales, offs, pos1, pos2, w1, lot, tgain, w2_words, w2_scales,
    sharp, thr, mgain, w3, ygain, out_0, out_1, out_2,
):
    nc = tc.nc
    with ExitStack() as ctx:
        sb = ctx.enter_context(tc.tile_pool(name="sb", bufs=1))
        ps = ctx.enter_context(tc.psum_pool(name="ps", bufs=1))

        def tile(shape, dtype, name, tag=""):
            return sb.tile(shape, dtype, name=name, tag=tag or name, align_bytes=64)

        def bank(shape, name, index):
            return ps.tile(shape, F32, name=name, tag="bank%d" % index)

        def deal_and_round(copy, dealt, raw, m0, m1):
            copy(
                out=dealt[:].rearrange("p (t m j) -> p m j t", t=PACK, j=PACK)[:, m0:m1],
                in_=raw[:].rearrange("p j (m t) -> p m j t", t=PACK)[:, m0:m1],
            )

        def planes_walk(planes):
            return planes.rearrange("p t (c i) -> p c t i", i=LINE)

        def woven_walk(woven):
            return woven.rearrange("p (c i t) -> p c t i", i=LINE, t=PACK)

        offs_sb = tile([P, S // PER_COLUMN], U16, "offs_sb")
        pos1_sb = tile([P, M // PER_COLUMN], U16, "pos1_sb")
        pos2_sb = tile([P, M // PER_COLUMN], U16, "pos2_sb")
        tscale = tile([P, T], U8, "tscale")
        w2w_raw = tile([P, 2 * H], U8, "w2w_raw")
        w2s_raw = tile([P, H], U8, "w2s_raw")
        nc.vector.memset(tscale[:].bitcast(I32), 0)
        nc.vector.memset(w2s_raw[:].bitcast(I32), 0)
        warm = tile([P, 2], F32, "warm")
        nc.gpsimd.memset(warm[:, 0:1], 0.0)
        nc.scalar.activation(out=warm[:, 1:2], in_=warm[:, 0:1], func=ACT.Sigmoid)
        twords = [tile([P, T], U32, "twords%d" % a) for a in range(PASSES)]
        w1_rows = w1.rearrange("(a p j) c -> a p j c", p=P, j=PACK)
        w1_raw = [tile([P, PACK, H], F32, "w1_raw%d" % a) for a in range(PASSES)]
        rowvec = {}

        def load_rowvec(name, vec):
            rowvec[name] = tile([P, PACK], F32, name + "_sb")
            nc.sync.dma_start(out=rowvec[name][:], in_=vec.rearrange("(p t) -> p t", t=PACK))

        def load_table(a):
            nc.sync.dma_start(
                out=twords[a][:].bitcast(I32),
                in_=tab_words[a].rearrange("p n t -> p (n t)").bitcast(I32),
            )

        nc.sync.dma_start(offs_sb[:], offs)
        load_table(0)
        nc.sync.dma_start(out=w1_raw[0][:], in_=w1_rows[0])
        for q in range(QUADS):
            nc.sync.dma_start(
                out=tscale[QUAD * q : QUAD * q + SCALE_ROWS * PASSES, :].bitcast(I32),
                in_=tab_scales[:, SCALE_ROWS * q : SCALE_ROWS * (q + 1), :].bitcast(I32),
            )
        nc.sync.dma_start(pos2_sb[:], pos2)
        nc.sync.dma_start(pos1_sb[:], pos1)
        nc.sync.dma_start(out=w1_raw[1][:], in_=w1_rows[1])
        load_table(1)
        load_table(2)
        nc.sync.dma_start(out=w1_raw[2][:], in_=w1_rows[2])
        nc.sync.dma_start(out=w2w_raw[:].bitcast(I32), in_=w2_words[0].bitcast(I32))
        for q in range(QUADS):
            nc.sync.dma_start(
                out=w2s_raw[QUAD * q : QUAD * q + SCALE_ROWS, :].bitcast(I32),
                in_=w2_scales[0, SCALE_ROWS * q : SCALE_ROWS * (q + 1), :].bitcast(I32),
            )
        lot_rows = lot.rearrange("(p t) s -> p t s", t=PACK)
        lot_sb = [tile([P, S], F32, "lot%d" % t) for t in range(PACK)]
        for t in range(PACK):
            nc.sync.dma_start(out=lot_sb[t][:], in_=lot_rows[:, t, :])
        load_rowvec("tgain", tgain)
        w3_raw = tile([P, PACK, H], F32, "w3_raw")
        nc.sync.dma_start(out=w3_raw[:], in_=w3.rearrange("(p j) c -> p j c", j=PACK))
        for name, vec in (("mgain", mgain), ("sharp", sharp), ("thr", thr), ("ygain", ygain)):
            load_rowvec(name, vec)

        vscale = tile([P, S], U8, "vscale")
        nc.vector.tensor_copy(vscale[:], tscale[:].indirect(offs_sb[:]))
        vwords = {0: tile([P, S], U32, "vwords0")}
        w1_codes = [tile([P, H], U32, "w1_codes%d" % a, tag="tscale" if a == 0 else "") for a in range(PASSES)]
        w1_scale = [tile([P, H], U8, "w1_scale%d" % a) for a in range(PASSES)]
        g_ps = {(u, t): bank([P, S_HALF], "g_ps%d%d" % (u, t), PACK * u + t) for u in range(2) for t in range(PACK)}

        def first_product(a, u, t):
            nc.tensor.matmul_mx(
                out=g_ps[u, t][:],
                lhsT=w1_codes[a][:, t * P : (t + 1) * P].bitcast(FP8X4),
                lhsT_scale=w1_scale[a][:, t * P : (t + 1) * P],
                rhs=vwords[a][:, u * S_HALF : (u + 1) * S_HALF].bitcast(FP8X4),
                rhs_scale=vscale[SCALE_ROWS * a : P, u * S_HALF : (u + 1) * S_HALF],
                start=(a == 0),
                stop=(a == PASSES - 1),
            )

        def pick_table(a, width):
            for c0 in range(0, S, width):
                entries = offs_sb[:, c0 // PER_COLUMN : (c0 + width) // PER_COLUMN]
                nc.vector.tensor_copy(vwords[a][:, c0 : c0 + width], twords[a][:].indirect(entries))

        def quantize_w1(a, width):
            w1_bf = tile([P, PACK * H], BF16, "w1_bf%d" % a)
            share = SCALAR_SHARE[a]
            deal_and_round(nc.scalar.copy, w1_bf, w1_raw[a], 0, share)
            if share < P:
                deal_and_round(nc.vector.tensor_copy, w1_bf, w1_raw[a], share, P)
            for c0 in range(0, H, width):
                nc.vector.quantize_mx(
                    out=w1_codes[a][:, c0 : c0 + width].bitcast(FP8X4),
                    scales=w1_scale[a][:, c0 : c0 + width],
                    in_=w1_bf[:, PACK * c0 : PACK * (c0 + width)],
                )

        pick_table(0, S)
        quantize_w1(0, H)
        for u in range(2):
            for t in range(PACK):
                first_product(0, u, t)
        quantize_w1(1, H)
        vwords[1] = tile([P, S], U32, "vwords1", tag="w1_bf1")
        pick_table(1, S_HALF)
        for u in range(2):
            for t in range(PACK):
                first_product(1, u, t)
        vwords[2] = tile([P, S], U32, "vwords2")
        pick_table(2, S)
        quantize_w1(2, P)
        for t in range(PACK):
            for u in range(2):
                first_product(2, u, t)

        w2w = tile([P, 2 * H], U8, "w2w")
        w2s = tile([P, H], U8, "w2s", tag="w1_bf2")
        nc.scalar.copy(
            out=w2w[:].bitcast(U16).rearrange("p (t m) -> p m t", t=PACK),
            in_=w2w_raw[:].bitcast(U16).rearrange("p (m t) -> p m t", t=PACK),
        )
        nc.vector.tensor_copy(
            out=w2s[:].rearrange("p (t m) -> p m t", t=PACK),
            in_=w2s_raw[:].rearrange("p (m t) -> p m t", t=PACK),
        )

        g = [tile([P, S], F32, "g%d" % t) for t in range(PACK)]
        tanh_g = [tile([P, PACK, S_HALF], F32, "tanh_g%d" % u, tag="w1_raw%d" % u) for u in range(2)]
        for t in range(PACK):
            for u in range(2):
                cols = slice(u * S_HALF, (u + 1) * S_HALF)
                nc.vector.tensor_tensor(out=g[t][:, cols], in0=g_ps[u, t][:], in1=lot_sb[t][:, cols], op=ALU.add)
                nc.scalar.activation(out=tanh_g[u][:, t, :], in_=g[t][:, cols], func=ACT.Tanh)

        w3_bf = tile([P, PACK * H], BF16, "w3_bf")
        deal_and_round(nc.scalar.copy, w3_bf, w3_raw, 0, P)

        h = [tile([P, S], F32, "h%d" % t) for t in range(PACK)]
        f_bf = {}

        def weave_f(quarter):
            f_bf[quarter] = tile([P, PACK * S_QUARTER], BF16, "f_bf%d" % quarter, tag="ring%d" % (quarter % 2))
            c0 = (quarter % 2) * S_QUARTER
            nc.vector.tensor_tensor(
                out=woven_walk(f_bf[quarter][:]),
                in0=planes_walk(tanh_g[quarter // 2][:, :, c0 : c0 + S_QUARTER]),
                in1=rowvec["tgain"][:].unsqueeze(1).unsqueeze(3).broadcast_to([P, S_QUARTER // LINE, PACK, LINE]),
                op=ALU.mult,
            )

        def second_product(quarter):
            f_codes = tile([P, S_QUARTER], U32, "f_codes%d" % quarter)
            f_scale = tile([P, S_QUARTER], U8, "f_scale%d" % quarter)
            nc.vector.quantize_mx(out=f_codes[:].bitcast(FP8X4), scales=f_scale[:], in_=f_bf[quarter][:])
            for pair in range(2):
                h_ps = bank([P, 2, S_QUARTER], "h_ps%d%d" % (quarter, pair), 2 * quarter + pair)
                for e in range(2):
                    t = 2 * pair + e
                    nc.tensor.matmul_mx(
                        out=h_ps[:, e, :],
                        lhsT=w2w[:, 2 * t * P : 2 * (t + 1) * P].bitcast(FP4X4),
                        lhsT_scale=w2s[:, t * P : (t + 1) * P],
                        rhs=f_codes[:].bitcast(FP8X4),
                        rhs_scale=f_scale[:],
                        start=True,
                        stop=True,
                    )
                for e in range(2):
                    nc.scalar.copy(
                        out=h[2 * pair + e][:, quarter * S_QUARTER : (quarter + 1) * S_QUARTER], in_=h_ps[:, e, :]
                    )

        weave_f(0)
        for quarter in range(1, 4):
            weave_f(quarter)
            second_product(quarter - 1)
        second_product(3)

        w3_codes = tile([P, H], U32, "w3_codes")
        w3_scale = tile([P, H], U8, "w3_scale")
        y_codes = tile([P, M], U32, "y_codes")
        y_scale = tile([P, M], U8, "y_scale")
        out_rows = out_0.rearrange("(p t) m -> p t m", t=PACK)
        out_words = out_1[0].rearrange("p m t -> p (m t)").bitcast(I32)
        control, z_ps, z = [], [], {}
        pieces = ((0, 2), (2, 3), (3, 4))

        def take_max(first, last):
            z[first] = tile([P, PACK, (last - first) * M_QUARTER], F32, "z%d" % first)
            for i in range(first, last):
                nc.vector.tensor_tensor(
                    out=z[first][:, :, (i - first) * M_QUARTER : (i - first + 1) * M_QUARTER],
                    in0=z_ps[i][:],
                    in1=control[i // 2][:, :, (i % 2) * M_QUARTER : (i % 2 + 1) * M_QUARTER],
                    op=ALU.max,
                )

        def pick_and_look(v):
            entries = slice(v * M_HALF // PER_COLUMN, (v + 1) * M_HALF // PER_COLUMN)
            control.append(tile([P, PACK, M_HALF], F32, "control%d" % v, tag="ring%d" % v))
            gained = tile([P, PACK, M_HALF], F32, "gained%d" % v)
            gate = tile([P, PACK, M_HALF], F32, "gate%d" % v)
            for t in range(PACK):
                nc.vector.tensor_copy(control[v][:, t, :], g[t][:].indirect(pos2_sb[:, entries]))
            for t in range(PACK):
                nc.scalar.activation(
                    out=gate[:, t, :],
                    in_=h[t][:].indirect(pos1_sb[:, entries]),
                    func=ACT.Sigmoid,
                    bias=rowvec["thr"][:, t : t + 1],
                    scale=rowvec["sharp"][:, t : t + 1],
                )
            return gate, gained

        def third_product(v, plain, gained, width, tag):
            d_bf = tile([P, PACK * M_HALF], BF16, "d_bf%d" % v, tag=tag)
            d_codes = tile([P, M_HALF], U32, "d_codes%d" % v)
            d_scale = tile([P, M_HALF], U8, "d_scale%d" % v)
            for m0 in range(0, M_HALF, width):
                nc.vector.tensor_tensor(
                    out=woven_walk(d_bf[:, PACK * m0 : PACK * (m0 + width)]),
                    in0=planes_walk(plain[:, :, m0 : m0 + width]),
                    in1=planes_walk(gained[:, :, m0 : m0 + width]),
                    op=ALU.mult,
                )
            for m0 in range(0, M_HALF, width):
                nc.vector.quantize_mx(
                    out=d_codes[:, m0 : m0 + width].bitcast(FP8X4),
                    scales=d_scale[:, m0 : m0 + width],
                    in_=d_bf[:, PACK * m0 : PACK * (m0 + width)],
                )
            for e in range(2):
                z_ps.append(bank([P, PACK, M_QUARTER], "z_ps%d%d" % (v, e), 2 * v + e))
                for t in range(PACK):
                    nc.tensor.matmul_mx(
                        out=z_ps[-1][:, t, :],
                        lhsT=w3_codes[:, t * P : (t + 1) * P].bitcast(FP8X4),
                        lhsT_scale=w3_scale[:, t * P : (t + 1) * P],
                        rhs=d_codes[:, e * M_QUARTER : (e + 1) * M_QUARTER].bitcast(FP8X4),
                        rhs_scale=d_scale[:, e * M_QUARTER : (e + 1) * M_QUARTER],
                        start=True,
                        stop=True,
                    )

        gate, gained = pick_and_look(0)
        for t in range(PACK):
            nc.vector.tensor_scalar(
                out=gained[:, t, :], in0=control[0][:, t, :], scalar1=rowvec["mgain"][:, t : t + 1], scalar2=None,
                op0=ALU.mult,
            )
        nc.vector.quantize_mx(out=w3_codes[:].bitcast(FP8X4), scales=w3_scale[:], in_=w3_bf[:])
        third_product(0, gate, gained, M_HALF, "d_bf0")

        gate, gained = pick_and_look(1)
        for t in range(PACK):
            nc.scalar.activation(
                out=gained[:, t, :], in_=gate[:, t, :], func=ACT.Copy, scale=rowvec["mgain"][:, t : t + 1]
            )
        take_max(*pieces[0])
        third_product(1, control[1], gained, M_QUARTER, "ring0")
        for first, last in pieces[1:]:
            take_max(first, last)

        for first, last in pieces:
            width = (last - first) * M_QUARTER
            cols = slice(first * M_QUARTER, last * M_QUARTER)
            y = tile([P, PACK, width], F32, "y%d" % first)
            for t in range(PACK):
                nc.scalar.activation(
                    out=y[:, t, :], in_=z[first][:, t, :], func=ACT.Copy, scale=rowvec["ygain"][:, t : t + 1]
                )
            nc.sync.dma_start(out=out_rows[:, :, cols], in_=y[:])
            y_bf = tile([P, PACK * width], BF16, "y_bf%d" % first)
            weave = nc.scalar.copy if first == 0 else nc.vector.tensor_copy
            weave(out=woven_walk(y_bf[:]), in_=planes_walk(y[:]))
            nc.vector.quantize_mx(out=y_codes[:, cols].bitcast(FP8X4), scales=y_scale[:, cols], in_=y_bf[:])
            if last % 2 == 0:
                half = slice(last * M_QUARTER - M_HALF, last * M_QUARTER)
                nc.sync.dma_start(out=out_words[:, half], in_=y_codes[:, half].bitcast(I32))
        for q in range(QUADS):
            queue = nc.sync if q % 2 else nc.scalar
            queue.dma_start(
                out=out_2[0, SCALE_ROWS * q : SCALE_ROWS * (q + 1), :].bitcast(I32),
                in_=y_scale[QUAD * q : QUAD * q + SCALE_ROWS, :].bitcast(I32),
            )
